import numpy as np, ml_dtypes
CORES = [12,28,44,60,3,19,35,51]
N = 8
import mx_ref
NC, D = 256, 5
SRC = [[0,1,2,6,7],[1,3,4,5,6],[3,4,5,6,7],[0,1,3,4,6],[0,1,2,5,6],[0,1,4,6,7],[0,3,4,5,7],[0,2,3,5,6]]
BF = ml_dtypes.bfloat16
def setup_inputs(rng):
    def f(*shape):
        return mx_ref.flush((rng.standard_normal(shape, dtype=np.float32) * np.exp2(rng.integers(-2, 3, shape[:-1] + (1,)))).astype(BF))
    return {"w": f(N, 128, D * 512), "x": f(N, 128, 4 * NC)}
def setup_inputs_blocks(rng):
    d = setup_inputs(rng)
    for k in ("w", "x"): d[k] = mx_ref.spread(d[k], rng, 2)
    return d
def setup_inputs_wide(rng):
    d = setup_inputs(rng)
    for k in ("w", "x"): d[k] = mx_ref.flush((d[k].astype(np.float32) * np.exp2(rng.integers(-8, 9, (N, 1, 1))).astype(np.float32)).astype(BF))
    return d
def setup_inputs_zeros(rng):
    d = setup_inputs(rng); v = d["x"].reshape(N, 128, -1, 4).copy()
    v[np.broadcast_to((rng.random((N, 1, v.shape[2], 1)) < 0.33), v.shape)] = 0
    d["x"] = v.reshape(d["x"].shape)
    return d
def reference(w, x):
    QX = [mx_ref.quantize(x[j]) for j in range(N)]
    y = np.zeros((N, 128, NC), np.float32)
    for r in range(N):
        for i in range(D):
            p = mx_ref.matmul(mx_ref.quantize(w[r][:, 512 * i:512 * i + 512]), QX[SRC[r][i]])
            y[r] = p if i == 0 else y[r] + p
    return {"y": y}

from concourse.bass import DstId, RemoteDMATransfer
from concourse.mybir import dt

NR, D, NC, WC = 8, 5, 256, 128

SCRATCH = {
    "xb": ("sbuf", [128, 4 * NC], "bfloat16"),
    "wb": ("sbuf", [128, 4 * WC * D], "bfloat16"),
    "wq": ("sbuf", [128, WC * D], "float8_e4m3fn_x4"),
    "ws": ("sbuf", [128, WC * D], "uint8"),
    "tq": ("sbuf", [128, NC * NR], "float8_e4m3fn_x4"),
    "ts": ("sbuf", [128, NC * NR], "uint8"),
    "acc": ("psum", [128, 512], "float32"),
    "yb": ("sbuf", [128, NC], "float32"),
}
SEMAPHORES = ["xl", "wl", "xqd", "wqd", "fs", "fc", "sent", "mm", "cp", "st"] + ["arr%d" % j for j in range(NR)]

HOP, FEED_NEAR, FEED_FAR = 1.0, 0.5, 0.75
_CACHE = {}


def _links(topo, chips, s, d):
    a, b, die = topo.chip(s), topo.chip(d), topo.die(s)
    if a == b:
        return []
    if topo.mates(a, b):
        return [("mate", a, die)]
    if topo.same_plane(a, b):
        return [("out", a, die), ("in", b, die)]
    m = [c for c in chips if topo.mates(a, c)][0]
    return [("mate", a, die), ("out", m, die), ("in", b, die)]


def _score(topo, cores, chips, jobs, who):
    load, sends = {}, {}
    for (j, r) in jobs:
        s = who[(j, r)]
        for p in _links(topo, chips, s, cores[r]):
            load[p] = load.get(p, 0) + 1
        sends.setdefault((j, s), []).append(r)
    when = {}
    for j in range(len(cores)):
        relays = [s for (jj, s) in sends if jj == j and s != cores[j]]
        feed = sum(FEED_NEAR if topo.die(s) == topo.die(cores[j]) else FEED_FAR for s in relays)
        for (jj, s), rs in sends.items():
            if jj == j:
                for r in rs:
                    when[(j, r)] = feed + len(rs) + (HOP if s == cores[j] else 2 * HOP)
    top = max(load.values())
    return (top, max(when.values()), sum(1 for v in load.values() if v == top), sum(v * v for v in load.values()),
            sum(1 for (j, s) in sends if s != cores[j])), when


def _plan(T, topo):
    if "plan" in _CACHE:
        return _CACHE["plan"]
    cores, src = list(T.cores), T.tables["SRC"]
    chips = sorted(set(topo.chip(c) for c in cores))
    jobs = [(j, r) for j in range(len(cores)) for r in range(len(cores)) if j in src[r] and r != j]
    span = max(cores) + 1
    while topo.chip(span) == topo.chip(max(cores)):
        span += 1
    opts = {}
    for (j, r) in jobs:
        same = [c for c in range(span) if topo.chip(c) == topo.chip(cores[j]) and (c == cores[j] or c not in cores)]
        opts[(j, r)] = [c for c in same if topo.may_write(c, cores[r])]
    who = {x: opts[x][0] for x in jobs}
    cur = _score(topo, cores, chips, jobs, who)[0]
    better = True
    while better:
        better = False
        for x in jobs:
            for o in opts[x]:
                old = who[x]
                if o == old:
                    continue
                who[x] = o
                new = _score(topo, cores, chips, jobs, who)[0]
                if new < cur:
                    cur, better = new, True
                else:
                    who[x] = old
        for x in jobs:
            for z in jobs:
                if z[0] != x[0] or z <= x:
                    continue
                for o in opts[x]:
                    for q in opts[z]:
                        old = (who[x], who[z])
                        who[x], who[z] = o, q
                        new = _score(topo, cores, chips, jobs, who)[0]
                        if new < cur:
                            cur, better = new, True
                        else:
                            who[x], who[z] = old
    when = _score(topo, cores, chips, jobs, who)[1]
    _CACHE["plan"] = (who, when)
    return _CACHE["plan"]


def _engines(topo, s, dsts):
    m = topo.mask(s, dsts[0])
    for d in dsts[1:]:
        m &= topo.mask(s, d)
    bits = [b for b in range(m.bit_length()) if (m >> b) & 1]
    n = 1
    while 2 * n <= len(bits) and 128 % (2 * n) == 0:
        n *= 2
    return sum(1 << b for b in bits[:n]), n


def _send(g, T, topo, core, j, dsts, sems):
    mask, n = _engines(topo, core, dsts)
    ids = [DstId(rid=topo.addr(d)[0], pnc=topo.addr(d)[1]) for d in dsts]
    a, b = NC * j, NC * (j + 1)
    for view, sem in ((T.ts[:, a:b], sems[0]), (T.tq[:, a:b].bitcast(dt.uint8), sems[1])):
        g.remote_dma_fused([RemoteDMATransfer(dst_ids=ids, dma_engine_mask=mask, remote_sem=sem, srcs=[view],
                                              dsts=[view for _ in dsts])], local_sem=T.sem.sent)
    return 2 * n


def rank_program(g, core, T, topo):
    who, when = _plan(T, topo)
    cores, src = list(T.cores), T.tables["SRC"]
    rank = T.rank_of(core)

    if rank is None:
        mine = sorted(x for x in who if who[x] == core)
        if not mine:
            return
        j = mine[0][0]
        dsts = [cores[r] for (_, r) in mine]
        fed = _engines(topo, cores[j], [s for s in sorted(set(who[x] for x in who if x[0] == j)) if s != cores[j]])[1]
        mask, n = _engines(topo, core, dsts)
        ids = [DstId(rid=topo.addr(d)[0], pnc=topo.addr(d)[1]) for d in dsts]
        a, b = NC * j, NC * (j + 1)
        for view, sem in ((T.ts[:, a:b], T.sem.fs), (T.tq[:, a:b].bitcast(dt.uint8), T.sem.fc)):
            g.wait_ge(sem, fed)
            g.remote_dma_fused([RemoteDMATransfer(dst_ids=ids, dma_engine_mask=mask, remote_sem=T.sem["arr%d" % j],
                                                  srcs=[view], dsts=[view for _ in dsts])], local_sem=T.sem.sent)
        g.wait_ge(T.sem.sent, 2 * n)
        return

    j = rank
    g.sync.dma_start(T.xb[:], T.x[:]).then_inc(T.sem.xl, 16)
    g.sync.dma_start(T.wb[:], T.w[:]).then_inc(T.sem.wl, 16)

    v = g.vector
    v.wait_ge(T.sem.xl, 16)
    v.quantize_mx(T.tq[:, NC * j:NC * (j + 1)], T.ts[:, NC * j:NC * (j + 1)], T.xb[:]).then_inc(T.sem.xqd, 1)
    v.wait_ge(T.sem.wl, 16)
    for i in range(D):
        v.quantize_mx(T.wq[:, WC * i:WC * (i + 1)], T.ws[:, WC * i:WC * (i + 1)],
                      T.wb[:, 4 * WC * i:4 * WC * (i + 1)]).then_inc(T.sem.wqd, 1)

    relays = sorted(set(who[x] for x in who if x[0] == j and who[x] != core))
    direct = [cores[r] for (jj, r) in sorted(who) if jj == j and who[(jj, r)] == core]
    g.wait_ge(T.sem.xqd, 1)
    left = 0
    if relays:
        left += _send(g, T, topo, core, j, relays, (T.sem.fs, T.sem.fc))
    if direct:
        left += _send(g, T, topo, core, j, direct, (T.sem["arr%d" % j], T.sem["arr%d" % j]))

    te = g.tensor
    te.wait_ge(T.sem.wqd, D)
    order = sorted(range(D), key=lambda i: (when.get((src[rank][i], rank), 0.0), i))
    for k, i in enumerate(order):
        s = src[rank][i]
        if s == rank:
            te.wait_ge(T.sem.xqd, 1)
        else:
            group = [cores[r] for (jj, r) in sorted(who) if jj == s and who[(jj, r)] == who[(s, rank)]]
            te.wait_ge(T.sem["arr%d" % s], 2 * _engines(topo, who[(s, rank)], group)[1])
        mm = te.matmul_mx(T.acc[:, 0:NC], T.wq[:, WC * i:WC * (i + 1)], T.ws[:, WC * i:WC * (i + 1)],
                          T.tq[:, NC * s:NC * (s + 1)], T.ts[:, NC * s:NC * (s + 1)], k == 0, k == D - 1)
    mm.then_inc(T.sem.mm, 1)

    v.wait_ge(T.sem.mm, 1)
    v.tensor_copy(T.yb[:], T.acc[:, 0:NC]).then_inc(T.sem.cp, 1)
    g.sync.wait_ge(T.sem.cp, 1)
    g.sync.dma_start(T.y[:], T.yb[:]).then_inc(T.sem.st, 16)
    g.sync.wait_ge(T.sem.st, 16)
    if left:
        g.wait_ge(T.sem.sent, left)
